import numpy as np
import ml_dtypes


def mxq(x, axis, fmt="e4m3"):
    dtype, down = {"e4m3": (ml_dtypes.float8_e4m3fn, 7), "e5m2": (ml_dtypes.float8_e5m2, 14)}[fmt]
    v = np.moveaxis(np.asarray(x, np.float32).astype(ml_dtypes.bfloat16).astype(np.float64), axis, -1)
    blocks = v.reshape(v.shape[:-1] + (-1, 32))
    amax = np.abs(blocks).max(-1, keepdims=True)
    byte = np.maximum(np.where(amax > 0, np.frexp(amax)[1] - 1 + 127, 0) - down, 1)
    scale = np.exp2(byte - 127.0)
    codes = (blocks / scale).astype(np.float32).astype(dtype).astype(np.float64)
    return np.moveaxis((codes * scale).reshape(v.shape), -1, axis)


WIDE = False


def mx_kscale(k):
    if not WIDE:
        return np.ones(k)
    levels = np.array([10, -10, 5, -5, 0])
    if k % 512:
        return np.exp2(np.random.permutation(np.resize(levels, k // 32))).repeat(32)
    a = np.empty((k // 512, 16))
    for p in range(k // 512):
        a[p, :8] = np.random.permutation(np.resize(levels, 8))
        for g in range(8):
            far = levels[np.abs(levels - a[p, g]) >= 10]
            a[p, g + 8] = far[np.random.randint(len(far))]
    return np.exp2(a.ravel()).repeat(32)


def f64(x):
    return np.asarray(x).astype(np.float64)


def striped(idx):
    return np.tile(idx.reshape(-1, 16).T, (8, 1)).astype(np.uint16)


def unstriped(offs):
    return offs[:16].T.reshape(-1).astype(np.int64)


def silu(v):
    return v / (1.0 + np.exp(-np.maximum(v, -700.0)))


K, T, D, S, V, N = 1024, 2048, 2, 768, 384, 128


def setup_inputs():
    n = np.random.standard_normal
    s = mx_kscale(K)[:, None]
    return {
        "xT": (n((K, T)) * s).astype(np.float32),
        "w": (n((K, N)) / np.sqrt(K) / s).astype(np.float32),
        "b": (0.3 * n((N, 1))).astype(np.float32),
        "gate": np.tile(np.random.uniform(0.2, 1.0, (D, 1, V)) / np.sqrt(D), (1, N, 1)).astype(np.float32),
        "offs": striped(np.random.permutation(T)[:S]),
        "pos1": striped(np.random.permutation(S)[:V]),
        "pos2": striped(np.random.permutation(S)[:V]),
    }


def reference(xT, w, b, gate, offs, pos1, pos2):
    idx = unstriped(offs)
    xq = mxq(f64(xT)[:, idx], 0, "e4m3")
    y = mxq(f64(w), 0, "e4m3").T @ xq
    y = silu(y + f64(b))
    return sum(f64(gate[d]) * y[:, unstriped(p)] for d, p in enumerate((pos1, pos2)))

@@ -1,0 +1,159 @@
+from contextlib import ExitStack
+
+import concourse.mybir as mybir
+
+K, T, D, S, V, N = 1024, 2048, 2, 768, 384, 128
+FLOPS = 2 * K * N * S
+
+F32 = mybir.dt.float32
+BF16 = mybir.dt.bfloat16
+U32 = mybir.dt.uint32
+U16 = mybir.dt.uint16
+U8 = mybir.dt.uint8
+FP8X4 = mybir.dt.float8_e4m3fn_x4
+SILU = mybir.ActivationFunctionType.Silu
+MULT = mybir.AluOpType.mult
+ADD = mybir.AluOpType.add
+
+P = 128
+PACK = 4
+PASSES = K // (P * PACK)
+CHUNK = 256
+LIST = 16
+
+
+def tile_picked_sub_lin_silu_sub_e_kernel(tc, xT, w, b, gate, offs, pos1, pos2, out):
+    nc = tc.nc
+    with ExitStack() as ctx:
+        keep = ctx.enter_context(tc.tile_pool(name="keep", bufs=1))
+        psum = ctx.enter_context(tc.psum_pool(name="psum", bufs=1))
+
+        offs_sb = keep.tile([P, S // LIST], U16, name="offs_sb")
+        pos_sb = [keep.tile([P, V // LIST], U16, name="pos_sb%d" % d) for d in range(D)]
+        planes = [keep.tile([P, T], F32, name="plane%d" % i) for i in range(PASSES * PACK)]
+        w_raw = keep.tile([P, PASSES, PACK, N], F32, name="w_raw")
+        bias = keep.tile([P, 1], F32, name="bias")
+        gate_sb = keep.tile([P, D, V], F32, name="gate_sb")
+
+        x_rows = xT.rearrange("(a p t) n -> a t p n", p=P, t=PACK)
+
+        def load_plane(i):
+            nc.sync.dma_start(out=planes[i][:], in_=x_rows[i // PACK, i % PACK])
+
+        load_plane(0)
+        nc.sync.dma_start(offs_sb[:], offs)
+        load_plane(1)
+        nc.sync.dma_start(out=w_raw[:], in_=w.rearrange("(a p t) n -> p a t n", p=P, t=PACK))
+        nc.sync.dma_start(out=bias[:], in_=b)
+        for i in range(2, PASSES * PACK):
+            load_plane(i)
+        nc.sync.dma_start(pos_sb[0][:], pos1)
+        nc.sync.dma_start(pos_sb[1][:], pos2)
+        nc.sync.dma_start(out=gate_sb[:], in_=gate.rearrange("d p v -> p d v"))
+
+        warm_in = keep.tile([P, 1], F32, name="warm_in")
+        warm_out = keep.tile([P, 1], F32, name="warm_out")
+        nc.vector.memset(warm_in[:], 0.0)
+        nc.scalar.activation(warm_out[:], warm_in[:], SILU)
+
+        picked = [keep.tile([P, PACK, S], F32, name="picked%d" % a) for a in range(PASSES)]
+        grouped = [keep.tile([P, S, PACK], BF16, name="grouped%d" % a, align_bytes=64) for a in range(PASSES)]
+        x_codes = [keep.tile([P, S], U32, name="x_codes%d" % a, align_bytes=64) for a in range(PASSES)]
+        x_scales = [keep.tile([P, S], U8, name="x_scales%d" % a, align_bytes=64) for a in range(PASSES)]
+        w_grouped = keep.tile([P, PASSES, N, PACK], BF16, name="w_grouped", align_bytes=64)
+        w_codes = keep.tile([P, PASSES * N], U32, name="w_codes", align_bytes=64)
+        w_scales = keep.tile([P, PASSES * N], U8, name="w_scales", align_bytes=64)
+        y = keep.tile([P, S], F32, name="y")
+
+        def window(a, t, lo, hi):
+            return planes[a * PACK + t][:].indirect(offs_sb[:, lo // LIST : hi // LIST])
+
+        def gather(a, t, lo, hi):
+            nc.vector.tensor_copy(picked[a][:, t, lo:hi], window(a, t, lo, hi))
+
+        def gather_in_place(a, t, lo, hi):
+            nc.vector.tensor_copy(grouped[a][:, lo:hi, t], window(a, t, lo, hi))
+
+        def interleave(a, t0, t1, lo, hi):
+            nc.scalar.copy(
+                grouped[a][:, lo:hi, t0:t1],
+                picked[a][:, t0:t1, lo:hi].rearrange("p t n -> p n t"),
+            )
+
+        def quantize(a, lo, hi):
+            nc.vector.quantize_mx(
+                out=x_codes[a][:, lo:hi].bitcast(FP8X4),
+                scales=x_scales[a][:, lo:hi],
+                in_=grouped[a][:, lo:hi, :].rearrange("p n t -> p (n t)"),
+            )
+
+        groups = [(0, 256), (512, 768), (256, 384), (384, 512)]
+        acc = [psum.tile([P, hi - lo], F32, name="acc%d" % lo) for lo, hi in groups]
+
+        def multiply(a, g):
+            lo, hi = groups[g]
+            nc.tensor.matmul_mx(
+                out=acc[g][:],
+                lhsT=w_codes[:, a * N : (a + 1) * N].bitcast(FP8X4),
+                lhsT_scale=w_scales[:, a * N : (a + 1) * N],
+                rhs=x_codes[a][:, lo:hi].bitcast(FP8X4),
+                rhs_scale=x_scales[a][:, lo:hi],
+                start=(a == 0),
+                stop=(a == PASSES - 1),
+            )
+
+        gather(0, 0, 0, S)
+        gather(0, 1, 0, S)
+        nc.scalar.copy(w_grouped[:], w_raw[:].rearrange("p a t n -> p a n t"))
+        gather(0, 2, 0, S)
+        nc.vector.quantize_mx(
+            out=w_codes[:].bitcast(FP8X4),
+            scales=w_scales[:],
+            in_=w_grouped[:].rearrange("p a n t -> p (a n t)"),
+        )
+        gather(0, 3, 0, S)
+        interleave(0, 0, PACK, 0, 512)
+        interleave(0, 0, PACK, 512, S)
+        gather(1, 0, 0, S)
+        quantize(0, 0, 512)
+        for lo in range(0, S, CHUNK):
+            gather(1, 1, lo, lo + CHUNK)
+            interleave(1, 0, 2, lo, lo + CHUNK)
+        quantize(0, 512, S)
+        for g in range(len(groups)):
+            multiply(0, g)
+
+        gather(1, 2, 0, 512)
+        gather_in_place(1, 2, 512, S)
+        for lo in (0, CHUNK):
+            gather(1, 3, lo, lo + CHUNK)
+            interleave(1, 2, PACK, lo, lo + CHUNK)
+        gather_in_place(1, 3, 512, S)
+        for g, (lo, hi) in enumerate(groups):
+            quantize(1, lo, hi)
+            multiply(1, g)
+            nc.scalar.activation(y[:, lo:hi], acc[g][:], SILU, bias=bias[:])
+
+        half = V // 2
+        terms = keep.tile([P, D, V], F32, name="terms")
+        result = keep.tile([P, V], F32, name="result")
+
+        def fetch(d, lo):
+            nc.vector.tensor_tensor(
+                terms[:, d, lo : lo + half],
+                y[:].indirect(pos_sb[d][:, lo // LIST : (lo + half) // LIST]),
+                gate_sb[:, d, lo : lo + half],
+                MULT,
+            )
+
+        def finish(lo):
+            cols = slice(lo, lo + half)
+            nc.vector.tensor_tensor(result[:, cols], terms[:, 0, cols], terms[:, 1, cols], ADD)
+            nc.sync.dma_start(out=out[:, cols], in_=result[:, cols])
+
+        fetch(0, 0)
+        fetch(1, 0)
+        fetch(0, half)
+        finish(0)
+        fetch(1, half)
+        finish(half)

@@ -40,13 +40,12 @@ def tile_picked_sub_lin_silu_sub_e_kernel(tc, xT, w, b, gate, offs, pos1, pos2, 
         def load_plane(i):
             nc.sync.dma_start(out=planes[i][:], in_=x_rows[i // PACK, i % PACK])
 
-        load_plane(0)
         nc.sync.dma_start(offs_sb[:], offs)
-        load_plane(1)
-        nc.sync.dma_start(out=w_raw[:], in_=w.rearrange("(a p t) n -> p a t n", p=P, t=PACK))
-        nc.sync.dma_start(out=bias[:], in_=b)
-        for i in range(2, PASSES * PACK):
+        for i in range(PASSES * PACK):
             load_plane(i)
+            if i == PACK:
+                nc.sync.dma_start(out=w_raw[:], in_=w.rearrange("(a p t) n -> p a t n", p=P, t=PACK))
+        nc.sync.dma_start(out=bias[:], in_=b)
         nc.sync.dma_start(pos_sb[0][:], pos1)
         nc.sync.dma_start(pos_sb[1][:], pos2)
         nc.sync.dma_start(out=gate_sb[:], in_=gate.rearrange("d p v -> p d v"))
@@ -80,6 +79,12 @@ def tile_picked_sub_lin_silu_sub_e_kernel(tc, xT, w, b, gate, offs, pos1, pos2, 
                 picked[a][:, t0:t1, lo:hi].rearrange("p t n -> p n t"),
             )
 
+        def interleave_all(dst, src):
+            nc.scalar.copy(
+                dst.rearrange("p (c i) t -> p c t i", i=4),
+                src.rearrange("p t (c i) -> p c t i", i=4),
+            )
+
         def quantize(a, lo, hi):
             nc.vector.quantize_mx(
                 out=x_codes[a][:, lo:hi].bitcast(FP8X4),
@@ -102,33 +107,36 @@ def tile_picked_sub_lin_silu_sub_e_kernel(tc, xT, w, b, gate, offs, pos1, pos2, 
                 stop=(a == PASSES - 1),
             )
 
+        def first_pair(a):
+            for lo in (2 * CHUNK, 0, CHUNK):
+                gather(a, 1, lo, lo + CHUNK)
+                interleave(a, 0, 2, lo, lo + CHUNK)
+
+        def second_pair(a):
+            gather(a, 2, 0, 2 * CHUNK)
+            gather_in_place(a, 2, 2 * CHUNK, S)
+            for lo in (0, CHUNK):
+                gather(a, 3, lo, lo + CHUNK)
+                interleave(a, 2, PACK, lo, lo + CHUNK)
+            gather_in_place(a, 3, 2 * CHUNK, S)
+
         gather(0, 0, 0, S)
-        gather(0, 1, 0, S)
-        nc.scalar.copy(w_grouped[:], w_raw[:].rearrange("p a t n -> p a n t"))
-        gather(0, 2, 0, S)
+        first_pair(0)
+        second_pair(0)
+        for lo in (0, 2 * CHUNK, CHUNK):
+            quantize(0, lo, lo + CHUNK)
+        gather(1, 0, 0, S)
+        for a in range(PASSES):
+            interleave_all(w_grouped[:, a], w_raw[:, a])
         nc.vector.quantize_mx(
             out=w_codes[:].bitcast(FP8X4),
             scales=w_scales[:],
             in_=w_grouped[:].rearrange("p a n t -> p (a n t)"),
         )
-        gather(0, 3, 0, S)
-        interleave(0, 0, PACK, 0, 512)
-        interleave(0, 0, PACK, 512, S)
-        gather(1, 0, 0, S)
-        quantize(0, 0, 512)
-        for lo in range(0, S, CHUNK):
-            gather(1, 1, lo, lo + CHUNK)
-            interleave(1, 0, 2, lo, lo + CHUNK)
-        quantize(0, 512, S)
         for g in range(len(groups)):
             multiply(0, g)
-
-        gather(1, 2, 0, 512)
-        gather_in_place(1, 2, 512, S)
-        for lo in (0, CHUNK):
-            gather(1, 3, lo, lo + CHUNK)
-            interleave(1, 2, PACK, lo, lo + CHUNK)
-        gather_in_place(1, 3, 512, S)
+        first_pair(1)
+        second_pair(1)
         for g, (lo, hi) in enumerate(groups):
             quantize(1, lo, hi)
             multiply(1, g)
@@ -138,22 +146,18 @@ def tile_picked_sub_lin_silu_sub_e_kernel(tc, xT, w, b, gate, offs, pos1, pos2, 
         terms = keep.tile([P, D, V], F32, name="terms")
         result = keep.tile([P, V], F32, name="result")
 
-        def fetch(d, lo):
+        def fetch(d, lo, hi):
             nc.vector.tensor_tensor(
-                terms[:, d, lo : lo + half],
-                y[:].indirect(pos_sb[d][:, lo // LIST : (lo + half) // LIST]),
-                gate_sb[:, d, lo : lo + half],
+                terms[:, d, lo:hi],
+                y[:].indirect(pos_sb[d][:, lo // LIST : hi // LIST]),
+                gate_sb[:, d, lo:hi],
                 MULT,
             )
 
-        def finish(lo):
+        fetch(0, 0, V)
+        fetch(1, 0, half)
+        fetch(1, half, V)
+        for queue, lo in ((nc.scalar, 0), (nc.sync, half)):
             cols = slice(lo, lo + half)
             nc.vector.tensor_tensor(result[:, cols], terms[:, 0, cols], terms[:, 1, cols], ADD)
-            nc.sync.dma_start(out=out[:, cols], in_=result[:, cols])
-
-        fetch(0, 0)
-        fetch(1, 0)
-        fetch(0, half)
-        finish(0)
-        fetch(1, half)
-        finish(half)
+            queue.dma_start(out=out[:, cols], in_=result[:, cols])

@@ -40,11 +40,14 @@ def tile_picked_sub_lin_silu_sub_e_kernel(tc, xT, w, b, gate, offs, pos1, pos2, 
         def load_plane(i):
             nc.sync.dma_start(out=planes[i][:], in_=x_rows[i // PACK, i % PACK])
 
-        nc.sync.dma_start(offs_sb[:], offs)
+        w_rows = w.rearrange("(a p t) n -> a p t n", p=P, t=PACK)
         for i in range(PASSES * PACK):
             load_plane(i)
+            if i == 0:
+                nc.sync.dma_start(offs_sb[:], offs)
             if i == PACK:
-                nc.sync.dma_start(out=w_raw[:], in_=w.rearrange("(a p t) n -> p a t n", p=P, t=PACK))
+                nc.sync.dma_start(out=w_raw[:, 0], in_=w_rows[0])
+        nc.sync.dma_start(out=w_raw[:, 1], in_=w_rows[1])
         nc.sync.dma_start(out=bias[:], in_=b)
         nc.sync.dma_start(pos_sb[0][:], pos1)
         nc.sync.dma_start(pos_sb[1][:], pos2)
@@ -92,7 +95,7 @@ def tile_picked_sub_lin_silu_sub_e_kernel(tc, xT, w, b, gate, offs, pos1, pos2, 
                 in_=grouped[a][:, lo:hi, :].rearrange("p n t -> p (n t)"),
             )
 
-        groups = [(0, 256), (512, 768), (256, 384), (384, 512)]
+        groups = [(lo, lo + 128) for lo in (0, 128, 512, 640, 256, 384)]
         acc = [psum.tile([P, hi - lo], F32, name="acc%d" % lo) for lo, hi in groups]
 
         def multiply(a, g):
@@ -112,37 +115,47 @@ def tile_picked_sub_lin_silu_sub_e_kernel(tc, xT, w, b, gate, offs, pos1, pos2, 
                 gather(a, 1, lo, lo + CHUNK)
                 interleave(a, 0, 2, lo, lo + CHUNK)
 
-        def second_pair(a):
+        def quantize_w(a):
+            nc.vector.quantize_mx(
+                out=w_codes[:, a * N : (a + 1) * N].bitcast(FP8X4),
+                scales=w_scales[:, a * N : (a + 1) * N],
+                in_=w_grouped[:, a].rearrange("p n t -> p (n t)"),
+            )
+
+        def third_plane(a):
             gather(a, 2, 0, 2 * CHUNK)
             gather_in_place(a, 2, 2 * CHUNK, S)
-            for lo in (0, CHUNK):
-                gather(a, 3, lo, lo + CHUNK)
-                interleave(a, 2, PACK, lo, lo + CHUNK)
-            gather_in_place(a, 3, 2 * CHUNK, S)
 
         gather(0, 0, 0, S)
         first_pair(0)
-        second_pair(0)
+        third_plane(0)
+        for lo in (0, CHUNK):
+            gather(0, 3, lo, lo + CHUNK)
+            interleave(0, 2, PACK, lo, lo + CHUNK)
+        gather_in_place(0, 3, 2 * CHUNK, S)
         for lo in (0, 2 * CHUNK, CHUNK):
             quantize(0, lo, lo + CHUNK)
         gather(1, 0, 0, S)
-        for a in range(PASSES):
-            interleave_all(w_grouped[:, a], w_raw[:, a])
-        nc.vector.quantize_mx(
-            out=w_codes[:].bitcast(FP8X4),
-            scales=w_scales[:],
-            in_=w_grouped[:].rearrange("p a n t -> p (a n t)"),
-        )
+        interleave_all(w_grouped[:, 0], w_raw[:, 0])
+        quantize_w(0)
         for g in range(len(groups)):
             multiply(0, g)
         first_pair(1)
-        second_pair(1)
+        third_plane(1)
+        gather(1, 3, 0, CHUNK)
+        interleave(1, 2, PACK, 0, CHUNK)
+        gather_in_place(1, 3, 2 * CHUNK, S)
+        interleave_all(w_grouped[:, 1], w_raw[:, 1])
+        gather(1, 3, CHUNK, 2 * CHUNK)
+        interleave(1, 2, PACK, CHUNK, CHUNK + 128)
+        interleave(1, 2, PACK, CHUNK + 128, 2 * CHUNK)
+        quantize_w(1)
         for g, (lo, hi) in enumerate(groups):
             quantize(1, lo, hi)
             multiply(1, g)
             nc.scalar.activation(y[:, lo:hi], acc[g][:], SILU, bias=bias[:])
 
-        half = V // 2
+        cut = V // 2
         terms = keep.tile([P, D, V], F32, name="terms")
         result = keep.tile([P, V], F32, name="result")
 
@@ -155,9 +168,8 @@ def tile_picked_sub_lin_silu_sub_e_kernel(tc, xT, w, b, gate, offs, pos1, pos2, 
             )
 
         fetch(0, 0, V)
-        fetch(1, 0, half)
-        fetch(1, half, V)
-        for queue, lo in ((nc.scalar, 0), (nc.sync, half)):
-            cols = slice(lo, lo + half)
+        fetch(1, 0, cut)
+        fetch(1, cut, V)
+        for queue, cols in ((nc.scalar, slice(0, cut)), (nc.sync, slice(cut, V))):
             nc.vector.tensor_tensor(result[:, cols], terms[:, 0, cols], terms[:, 1, cols], ADD)
             queue.dma_start(out=out[:, cols], in_=result[:, cols])

@@ -170,6 +170,6 @@ def tile_picked_sub_lin_silu_sub_e_kernel(tc, xT, w, b, gate, offs, pos1, pos2, 
         fetch(0, 0, V)
         fetch(1, 0, cut)
         fetch(1, cut, V)
-        for queue, cols in ((nc.scalar, slice(0, cut)), (nc.sync, slice(cut, V))):
+        for queue, cols in ((nc.sync, slice(0, cut)), (nc.sync, slice(cut, V))):
             nc.vector.tensor_tensor(result[:, cols], terms[:, 0, cols], terms[:, 1, cols], ADD)
             queue.dma_start(out=out[:, cols], in_=result[:, cols])

@@ -19,6 +19,7 @@ P = 128
 PACK = 4
 PASSES = K // (P * PACK)
 CHUNK = 256
+GROUP = 128
 LIST = 16
 
 
@@ -31,23 +32,19 @@ def tile_picked_sub_lin_silu_sub_e_kernel(tc, xT, w, b, gate, offs, pos1, pos2, 
         offs_sb = keep.tile([P, S // LIST], U16, name="offs_sb")
         pos_sb = [keep.tile([P, V // LIST], U16, name="pos_sb%d" % d) for d in range(D)]
         planes = [keep.tile([P, T], F32, name="plane%d" % i) for i in range(PASSES * PACK)]
-        w_raw = keep.tile([P, PASSES, PACK, N], F32, name="w_raw")
+        w_raw = [keep.tile([P, PACK, N], F32, name="w_raw%d" % a, tag="w_raw%d" % a, align_bytes=64) for a in range(PASSES)]
         bias = keep.tile([P, 1], F32, name="bias")
         gate_sb = keep.tile([P, D, V], F32, name="gate_sb")
 
         x_rows = xT.rearrange("(a p t) n -> a t p n", p=P, t=PACK)
-
-        def load_plane(i):
-            nc.sync.dma_start(out=planes[i][:], in_=x_rows[i // PACK, i % PACK])
-
         w_rows = w.rearrange("(a p t) n -> a p t n", p=P, t=PACK)
         for i in range(PASSES * PACK):
-            load_plane(i)
+            nc.sync.dma_start(out=planes[i][:], in_=x_rows[i // PACK, i % PACK])
             if i == 0:
                 nc.sync.dma_start(offs_sb[:], offs)
             if i == PACK:
-                nc.sync.dma_start(out=w_raw[:, 0], in_=w_rows[0])
-        nc.sync.dma_start(out=w_raw[:, 1], in_=w_rows[1])
+                nc.sync.dma_start(out=w_raw[0][:], in_=w_rows[0])
+        nc.sync.dma_start(out=w_raw[1][:], in_=w_rows[1])
         nc.sync.dma_start(out=bias[:], in_=b)
         nc.sync.dma_start(pos_sb[0][:], pos1)
         nc.sync.dma_start(pos_sb[1][:], pos2)
@@ -61,59 +58,39 @@ def tile_picked_sub_lin_silu_sub_e_kernel(tc, xT, w, b, gate, offs, pos1, pos2, 
         picked = [keep.tile([P, PACK, S], F32, name="picked%d" % a) for a in range(PASSES)]
         grouped = [keep.tile([P, S, PACK], BF16, name="grouped%d" % a, align_bytes=64) for a in range(PASSES)]
         x_codes = [keep.tile([P, S], U32, name="x_codes%d" % a, align_bytes=64) for a in range(PASSES)]
-        x_scales = [keep.tile([P, S], U8, name="x_scales%d" % a, align_bytes=64) for a in range(PASSES)]
         w_grouped = keep.tile([P, PASSES, N, PACK], BF16, name="w_grouped", align_bytes=64)
         w_codes = keep.tile([P, PASSES * N], U32, name="w_codes", align_bytes=64)
         w_scales = keep.tile([P, PASSES * N], U8, name="w_scales", align_bytes=64)
         y = keep.tile([P, S], F32, name="y")
 
-        def window(a, t, lo, hi):
-            return planes[a * PACK + t][:].indirect(offs_sb[:, lo // LIST : hi // LIST])
-
         def gather(a, t, lo, hi):
-            nc.vector.tensor_copy(picked[a][:, t, lo:hi], window(a, t, lo, hi))
+            window = planes[a * PACK + t][:].indirect(offs_sb[:, lo // LIST : hi // LIST])
+            nc.vector.tensor_copy(picked[a][:, t, lo:hi], window)
 
-        def gather_in_place(a, t, lo, hi):
-            nc.vector.tensor_copy(grouped[a][:, lo:hi, t], window(a, t, lo, hi))
-
-        def interleave(a, t0, t1, lo, hi):
+        def interleave(a, t0, lo, hi):
             nc.scalar.copy(
-                grouped[a][:, lo:hi, t0:t1],
-                picked[a][:, t0:t1, lo:hi].rearrange("p t n -> p n t"),
+                grouped[a][:, lo:hi, t0 : t0 + 2],
+                picked[a][:, t0 : t0 + 2, lo:hi].rearrange("p t n -> p n t"),
             )
 
-        def interleave_all(dst, src):
-            nc.scalar.copy(
-                dst.rearrange("p (c i) t -> p c t i", i=4),
-                src.rearrange("p t (c i) -> p c t i", i=4),
+        def pair(a, t0):
+            gather(a, t0, 0, S)
+            for lo in range(0, S, CHUNK):
+                gather(a, t0 + 1, lo, lo + CHUNK)
+                interleave(a, t0, lo, lo + CHUNK)
+
+        def w_views(a):
+            return (
+                w_grouped[:, a].rearrange("p (c i) t -> p c t i", i=4),
+                w_raw[a][:].rearrange("p t (c i) -> p c t i", i=4),
             )
 
-        def quantize(a, lo, hi):
+        def quantize(a, scales, lo, hi):
             nc.vector.quantize_mx(
                 out=x_codes[a][:, lo:hi].bitcast(FP8X4),
-                scales=x_scales[a][:, lo:hi],
+                scales=scales[:, lo:hi],
                 in_=grouped[a][:, lo:hi, :].rearrange("p n t -> p (n t)"),
             )
-
-        groups = [(lo, lo + 128) for lo in (0, 128, 512, 640, 256, 384)]
-        acc = [psum.tile([P, hi - lo], F32, name="acc%d" % lo) for lo, hi in groups]
-
-        def multiply(a, g):
-            lo, hi = groups[g]
-            nc.tensor.matmul_mx(
-                out=acc[g][:],
-                lhsT=w_codes[:, a * N : (a + 1) * N].bitcast(FP8X4),
-                lhsT_scale=w_scales[:, a * N : (a + 1) * N],
-                rhs=x_codes[a][:, lo:hi].bitcast(FP8X4),
-                rhs_scale=x_scales[a][:, lo:hi],
-                start=(a == 0),
-                stop=(a == PASSES - 1),
-            )
-
-        def first_pair(a):
-            for lo in (2 * CHUNK, 0, CHUNK):
-                gather(a, 1, lo, lo + CHUNK)
-                interleave(a, 0, 2, lo, lo + CHUNK)
 
         def quantize_w(a):
             nc.vector.quantize_mx(
@@ -122,38 +99,55 @@ def tile_picked_sub_lin_silu_sub_e_kernel(tc, xT, w, b, gate, offs, pos1, pos2, 
                 in_=w_grouped[:, a].rearrange("p n t -> p (n t)"),
             )
 
-        def third_plane(a):
-            gather(a, 2, 0, 2 * CHUNK)
-            gather_in_place(a, 2, 2 * CHUNK, S)
+        acc = [psum.tile([P, GROUP], F32, name="acc%d" % g) for g in range(S // GROUP)]
 
-        gather(0, 0, 0, S)
-        first_pair(0)
-        third_plane(0)
-        for lo in (0, CHUNK):
-            gather(0, 3, lo, lo + CHUNK)
-            interleave(0, 2, PACK, lo, lo + CHUNK)
-        gather_in_place(0, 3, 2 * CHUNK, S)
-        for lo in (0, 2 * CHUNK, CHUNK):
-            quantize(0, lo, lo + CHUNK)
-        gather(1, 0, 0, S)
-        interleave_all(w_grouped[:, 0], w_raw[:, 0])
+        def multiply(a, scales, g):
+            cols = slice(g * GROUP, (g + 1) * GROUP)
+            nc.tensor.matmul_mx(
+                out=acc[g][:],
+                lhsT=w_codes[:, a * N : (a + 1) * N].bitcast(FP8X4),
+                lhsT_scale=w_scales[:, a * N : (a + 1) * N],
+                rhs=x_codes[a][:, cols].bitcast(FP8X4),
+                rhs_scale=scales[:, cols],
+                start=(a == 0),
+                stop=(a == PASSES - 1),
+            )
+
+        pair(0, 0)
+        pair(0, 2)
+        pair(1, 0)
+        nc.scalar.copy(*w_views(0))
+        scales0 = keep.tile([P, S], U8, name="x_scales0", tag="w_raw0", align_bytes=64)
         quantize_w(0)
-        for g in range(len(groups)):
-            multiply(0, g)
-        first_pair(1)
-        third_plane(1)
+        quantize(0, scales0, 0, 2 * CHUNK)
+        quantize(0, scales0, 2 * CHUNK, S)
+        for g in range(S // GROUP):
+            multiply(0, scales0, g)
+
+        scales1 = keep.tile([P, S], U8, name="x_scales1", align_bytes=64)
+        direct = slice(2 * CHUNK, S)
+        gather(1, 2, direct.start, direct.stop)
+        nc.scalar.copy(
+            grouped[1][:, direct, 2:PACK],
+            picked[1][:, 2:3, direct].rearrange("p t n -> p n t").to_broadcast([P, CHUNK, 2]),
+        )
+        gather(1, 2, 0, direct.start)
         gather(1, 3, 0, CHUNK)
-        interleave(1, 2, PACK, 0, CHUNK)
-        gather_in_place(1, 3, 2 * CHUNK, S)
-        interleave_all(w_grouped[:, 1], w_raw[:, 1])
+        interleave(1, 2, 0, CHUNK)
+        nc.vector.tensor_copy(
+            grouped[1][:, direct, 3],
+            planes[PACK + 3][:].indirect(offs_sb[:, direct.start // LIST : direct.stop // LIST]),
+        )
+        nc.scalar.copy(*w_views(1))
         gather(1, 3, CHUNK, 2 * CHUNK)
-        interleave(1, 2, PACK, CHUNK, CHUNK + 128)
-        interleave(1, 2, PACK, CHUNK + 128, 2 * CHUNK)
+        interleave(1, 2, CHUNK, CHUNK + GROUP)
+        interleave(1, 2, CHUNK + GROUP, 2 * CHUNK)
         quantize_w(1)
-        for g, (lo, hi) in enumerate(groups):
-            quantize(1, lo, hi)
-            multiply(1, g)
-            nc.scalar.activation(y[:, lo:hi], acc[g][:], SILU, bias=bias[:])
+        for g in (0, 1, 4, 5, 2, 3):
+            cols = slice(g * GROUP, (g + 1) * GROUP)
+            quantize(1, scales1, cols.start, cols.stop)
+            multiply(1, scales1, g)
+            nc.scalar.activation(y[:, cols], acc[g][:], SILU, bias=bias[:])
 
         cut = V // 2
         terms = keep.tile([P, D, V], F32, name="terms")

@@ -149,9 +149,9 @@ def tile_picked_sub_lin_silu_sub_e_kernel(tc, xT, w, b, gate, offs, pos1, pos2, 
             multiply(1, scales1, g)
             nc.scalar.activation(y[:, cols], acc[g][:], SILU, bias=bias[:])
 
-        cut = V // 2
         terms = keep.tile([P, D, V], F32, name="terms")
         result = keep.tile([P, V], F32, name="result")
+        piece = V // 3
 
         def fetch(d, lo, hi):
             nc.vector.tensor_tensor(
@@ -161,9 +161,15 @@ def tile_picked_sub_lin_silu_sub_e_kernel(tc, xT, w, b, gate, offs, pos1, pos2, 
                 MULT,
             )
 
-        fetch(0, 0, V)
-        fetch(1, 0, cut)
-        fetch(1, cut, V)
-        for queue, cols in ((nc.sync, slice(0, cut)), (nc.sync, slice(cut, V))):
-            nc.vector.tensor_tensor(result[:, cols], terms[:, 0, cols], terms[:, 1, cols], ADD)
-            queue.dma_start(out=out[:, cols], in_=result[:, cols])
+        def add_and_store(lo, hi):
+            nc.vector.tensor_tensor(result[:, lo:hi], terms[:, 0, lo:hi], terms[:, 1, lo:hi], ADD)
+            nc.sync.dma_start(out=out[:, lo:hi], in_=result[:, lo:hi])
+
+        fetch(0, 0, piece)
+        fetch(1, 0, piece)
+        fetch(0, piece, V)
+        add_and_store(0, piece)
+        fetch(1, piece, 2 * piece)
+        fetch(1, 2 * piece, V)
+        add_and_store(piece, 2 * piece)
+        add_and_store(2 * piece, V)

@@ -55,7 +55,7 @@ def tile_picked_sub_lin_silu_sub_e_kernel(tc, xT, w, b, gate, offs, pos1, pos2, 
         nc.vector.memset(warm_in[:], 0.0)
         nc.scalar.activation(warm_out[:], warm_in[:], SILU)
 
-        picked = [keep.tile([P, PACK, S], F32, name="picked%d" % a) for a in range(PASSES)]
+        picked = [keep.tile([P, PACK, S], BF16, name="picked%d" % a) for a in range(PASSES)]
         grouped = [keep.tile([P, S, PACK], BF16, name="grouped%d" % a, align_bytes=64) for a in range(PASSES)]
         x_codes = [keep.tile([P, S], U32, name="x_codes%d" % a, align_bytes=64) for a in range(PASSES)]
         w_grouped = keep.tile([P, PASSES, N, PACK], BF16, name="w_grouped", align_bytes=64)
@@ -67,8 +67,8 @@ def tile_picked_sub_lin_silu_sub_e_kernel(tc, xT, w, b, gate, offs, pos1, pos2, 
             window = planes[a * PACK + t][:].indirect(offs_sb[:, lo // LIST : hi // LIST])
             nc.vector.tensor_copy(picked[a][:, t, lo:hi], window)
 
-        def interleave(a, t0, lo, hi):
-            nc.scalar.copy(
+        def interleave(a, t0, lo, hi, copy=nc.scalar.copy):
+            copy(
                 grouped[a][:, lo:hi, t0 : t0 + 2],
                 picked[a][:, t0 : t0 + 2, lo:hi].rearrange("p t n -> p n t"),
             )
@@ -132,8 +132,9 @@ def tile_picked_sub_lin_silu_sub_e_kernel(tc, xT, w, b, gate, offs, pos1, pos2, 
             picked[1][:, 2:3, direct].rearrange("p t n -> p n t").to_broadcast([P, CHUNK, 2]),
         )
         gather(1, 2, 0, direct.start)
-        gather(1, 3, 0, CHUNK)
-        interleave(1, 2, 0, CHUNK)
+        for lo in (0, GROUP):
+            gather(1, 3, lo, lo + GROUP)
+            interleave(1, 2, lo, lo + GROUP)
         nc.vector.tensor_copy(
             grouped[1][:, direct, 3],
             planes[PACK + 3][:].indirect(offs_sb[:, direct.start // LIST : direct.stop // LIST]),

@@ -126,12 +126,11 @@ def tile_picked_sub_lin_silu_sub_e_kernel(tc, xT, w, b, gate, offs, pos1, pos2, 
 
         scales1 = keep.tile([P, S], U8, name="x_scales1", align_bytes=64)
         direct = slice(2 * CHUNK, S)
-        gather(1, 2, direct.start, direct.stop)
-        nc.scalar.copy(
-            grouped[1][:, direct, 2:PACK],
-            picked[1][:, 2:3, direct].rearrange("p t n -> p n t").to_broadcast([P, CHUNK, 2]),
-        )
         gather(1, 2, 0, direct.start)
+        nc.vector.tensor_copy(
+            grouped[1][:, direct, 2],
+            planes[PACK + 2][:].indirect(offs_sb[:, direct.start // LIST : direct.stop // LIST]),
+        )
         for lo in (0, GROUP):
             gather(1, 3, lo, lo + GROUP)
             interleave(1, 2, lo, lo + GROUP)

@@ -31,8 +31,12 @@ def tile_picked_sub_lin_silu_sub_e_kernel(tc, xT, w, b, gate, offs, pos1, pos2, 
 
         offs_sb = keep.tile([P, S // LIST], U16, name="offs_sb")
         pos_sb = [keep.tile([P, V // LIST], U16, name="pos_sb%d" % d) for d in range(D)]
-        planes = [keep.tile([P, T], F32, name="plane%d" % i) for i in range(PASSES * PACK)]
-        w_raw = [keep.tile([P, PACK, N], F32, name="w_raw%d" % a, tag="w_raw%d" % a, align_bytes=64) for a in range(PASSES)]
+        planes = [keep.tile([P, T], F32, name="plane%d" % i, tag="plane%d" % i, align_bytes=64) for i in range(PASSES * PACK)]
+        half = S // 2
+        stage = keep.tile([P, half // 2 + PACK * N], F32, name="stage", align_bytes=64)
+        last_pair = stage[:].bitcast(BF16)[:, 0 : 2 * half].rearrange("p (t n) -> p t n", t=2)
+        w_raw1 = keep.tile([P, PACK, N], F32, name="w_raw1", tag="w_raw1", align_bytes=64)
+        w_raw = [stage[:, half // 2 :].rearrange("p (t n) -> p t n", t=PACK), w_raw1[:]]
         bias = keep.tile([P, 1], F32, name="bias")
         gate_sb = keep.tile([P, D, V], F32, name="gate_sb")
 
@@ -42,9 +46,8 @@ def tile_picked_sub_lin_silu_sub_e_kernel(tc, xT, w, b, gate, offs, pos1, pos2, 
             nc.sync.dma_start(out=planes[i][:], in_=x_rows[i // PACK, i % PACK])
             if i == 0:
                 nc.sync.dma_start(offs_sb[:], offs)
-            if i == PACK:
-                nc.sync.dma_start(out=w_raw[0][:], in_=w_rows[0])
-        nc.sync.dma_start(out=w_raw[1][:], in_=w_rows[1])
+        for a in range(PASSES):
+            nc.sync.dma_start(out=w_raw[a], in_=w_rows[a])
         nc.sync.dma_start(out=bias[:], in_=b)
         nc.sync.dma_start(pos_sb[0][:], pos1)
         nc.sync.dma_start(pos_sb[1][:], pos2)
@@ -82,7 +85,7 @@ def tile_picked_sub_lin_silu_sub_e_kernel(tc, xT, w, b, gate, offs, pos1, pos2, 
         def w_views(a):
             return (
                 w_grouped[:, a].rearrange("p (c i) t -> p c t i", i=4),
-                w_raw[a][:].rearrange("p t (c i) -> p c t i", i=4),
+                w_raw[a].rearrange("p t (c i) -> p c t i", i=4),
             )
 
         def quantize(a, scales, lo, hi):
@@ -99,10 +102,11 @@ def tile_picked_sub_lin_silu_sub_e_kernel(tc, xT, w, b, gate, offs, pos1, pos2, 
                 in_=w_grouped[:, a].rearrange("p n t -> p (n t)"),
             )
 
-        acc = [psum.tile([P, GROUP], F32, name="acc%d" % g) for g in range(S // GROUP)]
+        groups = [slice(384, 512), slice(512, 768), slice(0, 128), slice(128, 256), slice(256, 384)]
+        acc = [psum.tile([P, c.stop - c.start], F32, name="acc%d" % g) for g, c in enumerate(groups)]
 
         def multiply(a, scales, g):
-            cols = slice(g * GROUP, (g + 1) * GROUP)
+            cols = groups[g]
             nc.tensor.matmul_mx(
                 out=acc[g][:],
                 lhsT=w_codes[:, a * N : (a + 1) * N].bitcast(FP8X4),
@@ -115,36 +119,37 @@ def tile_picked_sub_lin_silu_sub_e_kernel(tc, xT, w, b, gate, offs, pos1, pos2, 
 
         pair(0, 0)
         pair(0, 2)
+        scales0a = keep.tile([P, S], U8, name="x_scales0a", align_bytes=64)
+        quantize(0, scales0a, 0, CHUNK)
         pair(1, 0)
-        nc.scalar.copy(*w_views(0))
-        scales0 = keep.tile([P, S], U8, name="x_scales0", tag="w_raw0", align_bytes=64)
-        quantize_w(0)
-        quantize(0, scales0, 0, 2 * CHUNK)
-        quantize(0, scales0, 2 * CHUNK, S)
-        for g in range(S // GROUP):
-            multiply(0, scales0, g)
+        scales0b = keep.tile([P, S], U8, name="x_scales0b", tag="plane4", align_bytes=64)
+        quantize(0, scales0b, CHUNK, S)
 
-        scales1 = keep.tile([P, S], U8, name="x_scales1", align_bytes=64)
-        direct = slice(2 * CHUNK, S)
-        gather(1, 2, 0, direct.start)
-        nc.vector.tensor_copy(
-            grouped[1][:, direct, 2],
-            planes[PACK + 2][:].indirect(offs_sb[:, direct.start // LIST : direct.stop // LIST]),
-        )
-        for lo in (0, GROUP):
-            gather(1, 3, lo, lo + GROUP)
-            interleave(1, 2, lo, lo + GROUP)
-        nc.vector.tensor_copy(
-            grouped[1][:, direct, 3],
-            planes[PACK + 3][:].indirect(offs_sb[:, direct.start // LIST : direct.stop // LIST]),
-        )
+        def staged(t, lo, hi):
+            window = planes[PACK + 2 + t][:].indirect(offs_sb[:, lo // LIST : hi // LIST])
+            nc.vector.tensor_copy(last_pair[:, t, lo:hi], window)
+
+        def in_place(t):
+            window = planes[PACK + t][:].indirect(offs_sb[:, half // LIST : S // LIST])
+            nc.vector.tensor_copy(grouped[1][:, half:S, t], window)
+
+        def place(lo, hi):
+            nc.scalar.copy(grouped[1][:, lo:hi, 2:4], last_pair[:, :, lo:hi].rearrange("p t n -> p n t"))
+
+        staged(0, 0, half)
+        in_place(2)
+        in_place(3)
+        nc.scalar.copy(*w_views(0))
+        quantize_w(0)
+        for g in range(len(groups)):
+            multiply(0, scales0a if groups[g].start < CHUNK else scales0b, g)
         nc.scalar.copy(*w_views(1))
-        gather(1, 3, CHUNK, 2 * CHUNK)
-        interleave(1, 2, CHUNK, CHUNK + GROUP)
-        interleave(1, 2, CHUNK + GROUP, 2 * CHUNK)
+        for lo in range(0, half, GROUP):
+            staged(1, lo, lo + GROUP)
+            place(lo, lo + GROUP)
+        scales1 = keep.tile([P, S], U8, name="x_scales1", tag="w_raw1", align_bytes=64)
         quantize_w(1)
-        for g in (0, 1, 4, 5, 2, 3):
-            cols = slice(g * GROUP, (g + 1) * GROUP)
+        for g, cols in enumerate(groups):
             quantize(1, scales1, cols.start, cols.stop)
             multiply(1, scales1, g)
             nc.scalar.activation(y[:, cols], acc[g][:], SILU, bias=bias[:])

@@ -33,10 +33,11 @@ def tile_picked_sub_lin_silu_sub_e_kernel(tc, xT, w, b, gate, offs, pos1, pos2, 
         pos_sb = [keep.tile([P, V // LIST], U16, name="pos_sb%d" % d) for d in range(D)]
         planes = [keep.tile([P, T], F32, name="plane%d" % i, tag="plane%d" % i, align_bytes=64) for i in range(PASSES * PACK)]
         half = S // 2
-        stage = keep.tile([P, half // 2 + PACK * N], F32, name="stage", align_bytes=64)
-        last_pair = stage[:].bitcast(BF16)[:, 0 : 2 * half].rearrange("p (t n) -> p t n", t=2)
+        wide = half + GROUP
+        stage = keep.tile([P, (wide + GROUP) // 2 + PACK * N], F32, name="stage", align_bytes=64)
+        last_pair = stage[:].bitcast(BF16)[:, 0 : 2 * wide].rearrange("p (t n) -> p t n", t=2)
         w_raw1 = keep.tile([P, PACK, N], F32, name="w_raw1", tag="w_raw1", align_bytes=64)
-        w_raw = [stage[:, half // 2 :].rearrange("p (t n) -> p t n", t=PACK), w_raw1[:]]
+        w_raw = [stage[:, (wide + GROUP) // 2 :].rearrange("p (t n) -> p t n", t=PACK), w_raw1[:]]
         bias = keep.tile([P, 1], F32, name="bias")
         gate_sb = keep.tile([P, D, V], F32, name="gate_sb")
 
@@ -76,11 +77,11 @@ def tile_picked_sub_lin_silu_sub_e_kernel(tc, xT, w, b, gate, offs, pos1, pos2, 
                 picked[a][:, t0 : t0 + 2, lo:hi].rearrange("p t n -> p n t"),
             )
 
-        def pair(a, t0):
+        def pair(a, t0, chunk):
             gather(a, t0, 0, S)
-            for lo in range(0, S, CHUNK):
-                gather(a, t0 + 1, lo, lo + CHUNK)
-                interleave(a, t0, lo, lo + CHUNK)
+            for lo in range(0, S, chunk):
+                gather(a, t0 + 1, lo, lo + chunk)
+                interleave(a, t0, lo, lo + chunk)
 
         def w_views(a):
             return (
@@ -102,7 +103,7 @@ def tile_picked_sub_lin_silu_sub_e_kernel(tc, xT, w, b, gate, offs, pos1, pos2, 
                 in_=w_grouped[:, a].rearrange("p n t -> p (n t)"),
             )
 
-        groups = [slice(384, 512), slice(512, 768), slice(0, 128), slice(128, 256), slice(256, 384)]
+        groups = [slice(0, 128), slice(384, 512), slice(512, 640), slice(640, 768), slice(128, 256), slice(256, 384)]
         acc = [psum.tile([P, c.stop - c.start], F32, name="acc%d" % g) for g, c in enumerate(groups)]
 
         def multiply(a, scales, g):
@@ -117,11 +118,11 @@ def tile_picked_sub_lin_silu_sub_e_kernel(tc, xT, w, b, gate, offs, pos1, pos2, 
                 stop=(a == PASSES - 1),
             )
 
-        pair(0, 0)
-        pair(0, 2)
+        pair(0, 0, half)
+        pair(0, 2, CHUNK)
         scales0a = keep.tile([P, S], U8, name="x_scales0a", align_bytes=64)
         quantize(0, scales0a, 0, CHUNK)
-        pair(1, 0)
+        pair(1, 0, half)
         scales0b = keep.tile([P, S], U8, name="x_scales0b", tag="plane4", align_bytes=64)
         quantize(0, scales0b, CHUNK, S)
 
@@ -129,22 +130,28 @@ def tile_picked_sub_lin_silu_sub_e_kernel(tc, xT, w, b, gate, offs, pos1, pos2, 
             window = planes[PACK + 2 + t][:].indirect(offs_sb[:, lo // LIST : hi // LIST])
             nc.vector.tensor_copy(last_pair[:, t, lo:hi], window)
 
-        def in_place(t):
-            window = planes[PACK + t][:].indirect(offs_sb[:, half // LIST : S // LIST])
-            nc.vector.tensor_copy(grouped[1][:, half:S, t], window)
+        def in_place(t, lo):
+            window = planes[PACK + t][:].indirect(offs_sb[:, lo // LIST : S // LIST])
+            nc.vector.tensor_copy(grouped[1][:, lo:S, t], window)
 
         def place(lo, hi):
             nc.scalar.copy(grouped[1][:, lo:hi, 2:4], last_pair[:, :, lo:hi].rearrange("p t n -> p n t"))
 
-        staged(0, 0, half)
-        in_place(2)
-        in_place(3)
+        staged(0, 0, wide)
+        nc.scalar.copy(
+            grouped[1][:, half:wide, 2:4],
+            last_pair[:, 0, half:wide].unsqueeze(2).to_broadcast([P, GROUP, 2]),
+        )
+        in_place(2, wide)
+        staged(1, 0, GROUP)
+        place(0, GROUP)
+        in_place(3, half)
         nc.scalar.copy(*w_views(0))
         quantize_w(0)
         for g in range(len(groups)):
             multiply(0, scales0a if groups[g].start < CHUNK else scales0b, g)
         nc.scalar.copy(*w_views(1))
-        for lo in range(0, half, GROUP):
+        for lo in range(GROUP, half, GROUP):
             staged(1, lo, lo + GROUP)
             place(lo, lo + GROUP)
         scales1 = keep.tile([P, S], U8, name="x_scales1", tag="w_raw1", align_bytes=64)

@@ -34,10 +34,10 @@ def tile_picked_sub_lin_silu_sub_e_kernel(tc, xT, w, b, gate, offs, pos1, pos2, 
         planes = [keep.tile([P, T], F32, name="plane%d" % i, tag="plane%d" % i, align_bytes=64) for i in range(PASSES * PACK)]
         half = S // 2
         wide = half + GROUP
-        stage = keep.tile([P, (wide + GROUP) // 2 + PACK * N], F32, name="stage", align_bytes=64)
+        stage = keep.tile([P, (wide + 2 * GROUP) // 2 + PACK * N], F32, name="stage", align_bytes=64)
         last_pair = stage[:].bitcast(BF16)[:, 0 : 2 * wide].rearrange("p (t n) -> p t n", t=2)
         w_raw1 = keep.tile([P, PACK, N], F32, name="w_raw1", tag="w_raw1", align_bytes=64)
-        w_raw = [stage[:, (wide + GROUP) // 2 :].rearrange("p (t n) -> p t n", t=PACK), w_raw1[:]]
+        w_raw = [stage[:, (wide + 2 * GROUP) // 2 :].rearrange("p (t n) -> p t n", t=PACK), w_raw1[:]]
         bias = keep.tile([P, 1], F32, name="bias")
         gate_sb = keep.tile([P, D, V], F32, name="gate_sb")
 
@@ -103,7 +103,7 @@ def tile_picked_sub_lin_silu_sub_e_kernel(tc, xT, w, b, gate, offs, pos1, pos2, 
                 in_=w_grouped[:, a].rearrange("p n t -> p (n t)"),
             )
 
-        groups = [slice(0, 128), slice(384, 512), slice(512, 640), slice(640, 768), slice(128, 256), slice(256, 384)]
+        groups = [slice(0, 128), slice(128, 256), slice(512, 640), slice(640, 768), slice(256, 384), slice(384, 512)]
         acc = [psum.tile([P, c.stop - c.start], F32, name="acc%d" % g) for g, c in enumerate(groups)]
 
         def multiply(a, scales, g):
@@ -138,20 +138,17 @@ def tile_picked_sub_lin_silu_sub_e_kernel(tc, xT, w, b, gate, offs, pos1, pos2, 
             nc.scalar.copy(grouped[1][:, lo:hi, 2:4], last_pair[:, :, lo:hi].rearrange("p t n -> p n t"))
 
         staged(0, 0, wide)
-        nc.scalar.copy(
-            grouped[1][:, half:wide, 2:4],
-            last_pair[:, 0, half:wide].unsqueeze(2).to_broadcast([P, GROUP, 2]),
-        )
         in_place(2, wide)
-        staged(1, 0, GROUP)
-        place(0, GROUP)
-        in_place(3, half)
-        nc.scalar.copy(*w_views(0))
+        for lo in (0, GROUP):
+            staged(1, lo, lo + GROUP)
+            place(lo, lo + GROUP)
+        in_place(3, wide)
+        nc.gpsimd.tensor_scalar(*w_views(0), 1.0, 0.0, MULT, ADD)
         quantize_w(0)
         for g in range(len(groups)):
             multiply(0, scales0a if groups[g].start < CHUNK else scales0b, g)
         nc.scalar.copy(*w_views(1))
-        for lo in range(GROUP, half, GROUP):
+        for lo in range(2 * GROUP, wide, GROUP):
             staged(1, lo, lo + GROUP)
             place(lo, lo + GROUP)
         scales1 = keep.tile([P, S], U8, name="x_scales1", tag="w_raw1", align_bytes=64)

@@ -12,15 +12,17 @@ U16 = mybir.dt.uint16
 U8 = mybir.dt.uint8
 FP8X4 = mybir.dt.float8_e4m3fn_x4
 SILU = mybir.ActivationFunctionType.Silu
+COPY = mybir.ActivationFunctionType.Copy
 MULT = mybir.AluOpType.mult
 ADD = mybir.AluOpType.add
 
 P = 128
 PACK = 4
 PASSES = K // (P * PACK)
-CHUNK = 256
 GROUP = 128
 LIST = 16
+HALF = S // 2
+THIRD = S // 3
 
 
 def tile_picked_sub_lin_silu_sub_e_kernel(tc, xT, w, b, gate, offs, pos1, pos2, out):
@@ -31,22 +33,26 @@ def tile_picked_sub_lin_silu_sub_e_kernel(tc, xT, w, b, gate, offs, pos1, pos2, 
 
         offs_sb = keep.tile([P, S // LIST], U16, name="offs_sb")
         pos_sb = [keep.tile([P, V // LIST], U16, name="pos_sb%d" % d) for d in range(D)]
-        planes = [keep.tile([P, T], F32, name="plane%d" % i, tag="plane%d" % i, align_bytes=64) for i in range(PASSES * PACK)]
-        half = S // 2
-        wide = half + GROUP
-        stage = keep.tile([P, (wide + 2 * GROUP) // 2 + PACK * N], F32, name="stage", align_bytes=64)
-        last_pair = stage[:].bitcast(BF16)[:, 0 : 2 * wide].rearrange("p (t n) -> p t n", t=2)
+        twin = [keep.tile([P, 2 * T], F32, name="twin%d" % j, align_bytes=64) for j in range(3)]
+        lone = [keep.tile([P, T], F32, name="lone%d" % j, align_bytes=64) for j in range(2)]
+        staged_n = S - THIRD
+        w_at = (staged_n + 2 * GROUP) // 2
+        stage = keep.tile([P, w_at + PACK * N], F32, name="stage", align_bytes=64)
+        last_pair = stage[:].bitcast(BF16)[:, 0 : 2 * staged_n].rearrange("p (t n) -> p t n", t=2)
         w_raw1 = keep.tile([P, PACK, N], F32, name="w_raw1", tag="w_raw1", align_bytes=64)
-        w_raw = [stage[:, (wide + 2 * GROUP) // 2 :].rearrange("p (t n) -> p t n", t=PACK), w_raw1[:]]
+        w_raw = [stage[:, w_at:].rearrange("p (t n) -> p t n", t=PACK), w_raw1[:]]
         bias = keep.tile([P, 1], F32, name="bias")
         gate_sb = keep.tile([P, D, V], F32, name="gate_sb")
 
+        x_pairs = xT.rearrange("(a p u t) n -> a u p (t n)", p=P, u=2, t=2)
         x_rows = xT.rearrange("(a p t) n -> a t p n", p=P, t=PACK)
         w_rows = w.rearrange("(a p t) n -> a p t n", p=P, t=PACK)
-        for i in range(PASSES * PACK):
-            nc.sync.dma_start(out=planes[i][:], in_=x_rows[i // PACK, i % PACK])
-            if i == 0:
-                nc.sync.dma_start(offs_sb[:], offs)
+        nc.sync.dma_start(out=twin[0][:], in_=x_pairs[0, 0])
+        nc.sync.dma_start(offs_sb[:], offs)
+        nc.sync.dma_start(out=twin[1][:], in_=x_pairs[0, 1])
+        nc.sync.dma_start(out=twin[2][:], in_=x_pairs[1, 0])
+        for j in range(2):
+            nc.sync.dma_start(out=lone[j][:], in_=x_rows[1, 2 + j])
         for a in range(PASSES):
             nc.sync.dma_start(out=w_raw[a], in_=w_rows[a])
         nc.sync.dma_start(out=bias[:], in_=b)
@@ -59,29 +65,24 @@ def tile_picked_sub_lin_silu_sub_e_kernel(tc, xT, w, b, gate, offs, pos1, pos2, 
         nc.vector.memset(warm_in[:], 0.0)
         nc.scalar.activation(warm_out[:], warm_in[:], SILU)
 
-        picked = [keep.tile([P, PACK, S], BF16, name="picked%d" % a) for a in range(PASSES)]
+        picked0 = keep.tile([P, 2, PACK, HALF], BF16, name="picked0")
+        picked1 = keep.tile([P, 3, 3, THIRD], BF16, name="picked1")
         grouped = [keep.tile([P, S, PACK], BF16, name="grouped%d" % a, align_bytes=64) for a in range(PASSES)]
         x_codes = [keep.tile([P, S], U32, name="x_codes%d" % a, align_bytes=64) for a in range(PASSES)]
+        scales0 = keep.tile([P, S], U8, name="x_scales0", align_bytes=64)
         w_grouped = keep.tile([P, PASSES, N, PACK], BF16, name="w_grouped", align_bytes=64)
         w_codes = keep.tile([P, PASSES * N], U32, name="w_codes", align_bytes=64)
         w_scales = keep.tile([P, PASSES * N], U8, name="w_scales", align_bytes=64)
         y = keep.tile([P, S], F32, name="y")
 
-        def gather(a, t, lo, hi):
-            window = planes[a * PACK + t][:].indirect(offs_sb[:, lo // LIST : hi // LIST])
-            nc.vector.tensor_copy(picked[a][:, t, lo:hi], window)
+        def entries(lo, hi):
+            return offs_sb[:, lo // LIST : hi // LIST]
 
-        def interleave(a, t0, lo, hi, copy=nc.scalar.copy):
-            copy(
-                grouped[a][:, lo:hi, t0 : t0 + 2],
-                picked[a][:, t0 : t0 + 2, lo:hi].rearrange("p t n -> p n t"),
-            )
+        def scalar_gather(dst, window, lo, hi):
+            nc.scalar.activation(dst, window.indirect(entries(lo, hi)), COPY)
 
-        def pair(a, t0, chunk):
-            gather(a, t0, 0, S)
-            for lo in range(0, S, chunk):
-                gather(a, t0 + 1, lo, lo + chunk)
-                interleave(a, t0, lo, lo + chunk)
+        def vector_gather(dst, window, lo, hi):
+            nc.vector.tensor_copy(dst, window.indirect(entries(lo, hi)))
 
         def w_views(a):
             return (
@@ -103,8 +104,9 @@ def tile_picked_sub_lin_silu_sub_e_kernel(tc, xT, w, b, gate, offs, pos1, pos2, 
                 in_=w_grouped[:, a].rearrange("p n t -> p (n t)"),
             )
 
-        groups = [slice(0, 128), slice(128, 256), slice(512, 640), slice(640, 768), slice(256, 384), slice(384, 512)]
-        acc = [psum.tile([P, c.stop - c.start], F32, name="acc%d" % g) for g, c in enumerate(groups)]
+        starts = [2 * GROUP, 3 * GROUP, 0, GROUP, 4 * GROUP, 5 * GROUP]
+        groups = [slice(s, s + GROUP) for s in starts]
+        acc = [psum.tile([P, GROUP], F32, name="acc%d" % g) for g in range(len(groups))]
 
         def multiply(a, scales, g):
             cols = groups[g]
@@ -118,39 +120,46 @@ def tile_picked_sub_lin_silu_sub_e_kernel(tc, xT, w, b, gate, offs, pos1, pos2, 
                 stop=(a == PASSES - 1),
             )
 
-        pair(0, 0, half)
-        pair(0, 2, CHUNK)
-        scales0a = keep.tile([P, S], U8, name="x_scales0a", align_bytes=64)
-        quantize(0, scales0a, 0, CHUNK)
-        pair(1, 0, half)
-        scales0b = keep.tile([P, S], U8, name="x_scales0b", tag="plane4", align_bytes=64)
-        quantize(0, scales0b, CHUNK, S)
+        for u in range(2):
+            for h in range(2):
+                scalar_gather(picked0[:, h, 2 * u, :], twin[u][:], h * HALF, (h + 1) * HALF)
+            vector_gather(picked0[:, :, 2 * u + 1, :], twin[u][:, T:], 0, S)
+        for h in range(2):
+            nc.vector.tensor_copy(
+                grouped[0][:, h * HALF : (h + 1) * HALF, :].rearrange("p (c i) t -> p c t i", i=4),
+                picked0[:, h].rearrange("p t (c i) -> p c t i", i=4),
+            )
+        for h in range(2):
+            quantize(0, scales0, h * HALF, (h + 1) * HALF)
 
-        def staged(t, lo, hi):
-            window = planes[PACK + 2 + t][:].indirect(offs_sb[:, lo // LIST : hi // LIST])
-            nc.vector.tensor_copy(last_pair[:, t, lo:hi], window)
+        for c in (1, 2, 0):
+            scalar_gather(picked1[:, c, 0, :], twin[2][:], c * THIRD, (c + 1) * THIRD)
+        vector_gather(picked1[:, :, 1, :], twin[2][:, T:], 0, S)
+        nc.vector.tensor_copy(
+            grouped[1][:, THIRD:S, 0:2].rearrange("p (c i) t -> p c i t", c=2),
+            picked1[:, 1:3, 0:2, :].rearrange("p c t i -> p c i t"),
+        )
+        scalar_gather(picked1[:, 0, 2, :], lone[0][:], 0, THIRD)
+        scalar_gather(last_pair[:, 0, :], lone[0][:], THIRD, S)
+        nc.vector.tensor_copy(grouped[1][:, 0:THIRD, 0:3], picked1[:, 0].rearrange("p t i -> p i t"))
 
-        def in_place(t, lo):
-            window = planes[PACK + t][:].indirect(offs_sb[:, lo // LIST : S // LIST])
-            nc.vector.tensor_copy(grouped[1][:, lo:S, t], window)
+        def staged(lo):
+            vector_gather(last_pair[:, 1, lo - THIRD : lo - THIRD + GROUP], lone[1][:], lo, lo + GROUP)
+            nc.scalar.copy(
+                grouped[1][:, lo : lo + GROUP, 2:4],
+                last_pair[:, :, lo - THIRD : lo - THIRD + GROUP].rearrange("p t n -> p n t"),
+            )
 
-        def place(lo, hi):
-            nc.scalar.copy(grouped[1][:, lo:hi, 2:4], last_pair[:, :, lo:hi].rearrange("p t n -> p n t"))
-
-        staged(0, 0, wide)
-        in_place(2, wide)
-        for lo in (0, GROUP):
-            staged(1, lo, lo + GROUP)
-            place(lo, lo + GROUP)
-        in_place(3, wide)
+        staged(2 * GROUP)
+        staged(3 * GROUP)
+        vector_gather(grouped[1][:, 0:THIRD, 3], lone[1][:], 0, THIRD)
         nc.gpsimd.tensor_scalar(*w_views(0), 1.0, 0.0, MULT, ADD)
         quantize_w(0)
         for g in range(len(groups)):
-            multiply(0, scales0a if groups[g].start < CHUNK else scales0b, g)
+            multiply(0, scales0, g)
         nc.scalar.copy(*w_views(1))
-        for lo in range(2 * GROUP, wide, GROUP):
-            staged(1, lo, lo + GROUP)
-            place(lo, lo + GROUP)
+        staged(4 * GROUP)
+        staged(5 * GROUP)
         scales1 = keep.tile([P, S], U8, name="x_scales1", tag="w_raw1", align_bytes=64)
         quantize_w(1)
         for g, cols in enumerate(groups):
@@ -158,27 +167,31 @@ def tile_picked_sub_lin_silu_sub_e_kernel(tc, xT, w, b, gate, offs, pos1, pos2, 
             multiply(1, scales1, g)
             nc.scalar.activation(y[:, cols], acc[g][:], SILU, bias=bias[:])
 
-        terms = keep.tile([P, D, V], F32, name="terms")
+        first = keep.tile([P, V], F32, name="first")
+        fetched = keep.tile([P, V], F32, name="fetched")
+        second = keep.tile([P, V], F32, name="second")
         result = keep.tile([P, V], F32, name="result")
         piece = V // 3
 
-        def fetch(d, lo, hi):
+        def fetch_first(lo, hi):
             nc.vector.tensor_tensor(
-                terms[:, d, lo:hi],
-                y[:].indirect(pos_sb[d][:, lo // LIST : hi // LIST]),
-                gate_sb[:, d, lo:hi],
-                MULT,
+                first[:, lo:hi], y[:].indirect(pos_sb[0][:, lo // LIST : hi // LIST]), gate_sb[:, 0, lo:hi], MULT
             )
 
+        def weigh_second(lo, hi):
+            nc.vector.tensor_tensor(second[:, lo:hi], fetched[:, lo:hi], gate_sb[:, 1, lo:hi], MULT)
+
         def add_and_store(lo, hi):
-            nc.vector.tensor_tensor(result[:, lo:hi], terms[:, 0, lo:hi], terms[:, 1, lo:hi], ADD)
+            nc.vector.tensor_tensor(result[:, lo:hi], first[:, lo:hi], second[:, lo:hi], ADD)
             nc.sync.dma_start(out=out[:, lo:hi], in_=result[:, lo:hi])
 
-        fetch(0, 0, piece)
-        fetch(1, 0, piece)
-        fetch(0, piece, V)
+        for lo, hi in ((0, piece), (piece, V)):
+            nc.scalar.activation(fetched[:, lo:hi], y[:].indirect(pos_sb[1][:, lo // LIST : hi // LIST]), COPY)
+        fetch_first(0, piece)
+        weigh_second(0, piece)
+        fetch_first(piece, 2 * piece)
         add_and_store(0, piece)
-        fetch(1, piece, 2 * piece)
-        fetch(1, 2 * piece, V)
+        weigh_second(piece, V)
+        fetch_first(2 * piece, V)
         add_and_store(piece, 2 * piece)
         add_and_store(2 * piece, V)

@@ -22,7 +22,8 @@ PASSES = K // (P * PACK)
 GROUP = 128
 LIST = 16
 HALF = S // 2
-THIRD = S // 3
+QUARTER = S // 4
+IN_PLACE = S // 2
 
 
 def tile_picked_sub_lin_silu_sub_e_kernel(tc, xT, w, b, gate, offs, pos1, pos2, out):
@@ -35,12 +36,9 @@ def tile_picked_sub_lin_silu_sub_e_kernel(tc, xT, w, b, gate, offs, pos1, pos2, 
         pos_sb = [keep.tile([P, V // LIST], U16, name="pos_sb%d" % d) for d in range(D)]
         twin = [keep.tile([P, 2 * T], F32, name="twin%d" % j, align_bytes=64) for j in range(3)]
         lone = [keep.tile([P, T], F32, name="lone%d" % j, align_bytes=64) for j in range(2)]
-        staged_n = S - THIRD
-        w_at = (staged_n + 2 * GROUP) // 2
-        stage = keep.tile([P, w_at + PACK * N], F32, name="stage", align_bytes=64)
-        last_pair = stage[:].bitcast(BF16)[:, 0 : 2 * staged_n].rearrange("p (t n) -> p t n", t=2)
-        w_raw1 = keep.tile([P, PACK, N], F32, name="w_raw1", tag="w_raw1", align_bytes=64)
-        w_raw = [stage[:, w_at:].rearrange("p (t n) -> p t n", t=PACK), w_raw1[:]]
+        staged_n = S - IN_PLACE
+        last_pair = keep.tile([P, 2, staged_n], BF16, name="last_pair")
+        w_raw = [keep.tile([P, PACK, N], F32, name="w_raw%d" % a, tag="w_raw%d" % a, align_bytes=64)[:] for a in range(PASSES)]
         bias = keep.tile([P, 1], F32, name="bias")
         gate_sb = keep.tile([P, D, V], F32, name="gate_sb")
 
@@ -49,12 +47,12 @@ def tile_picked_sub_lin_silu_sub_e_kernel(tc, xT, w, b, gate, offs, pos1, pos2, 
         w_rows = w.rearrange("(a p t) n -> a p t n", p=P, t=PACK)
         nc.sync.dma_start(out=twin[0][:], in_=x_pairs[0, 0])
         nc.sync.dma_start(offs_sb[:], offs)
+        nc.sync.dma_start(out=w_raw[0], in_=w_rows[0])
         nc.sync.dma_start(out=twin[1][:], in_=x_pairs[0, 1])
         nc.sync.dma_start(out=twin[2][:], in_=x_pairs[1, 0])
         for j in range(2):
             nc.sync.dma_start(out=lone[j][:], in_=x_rows[1, 2 + j])
-        for a in range(PASSES):
-            nc.sync.dma_start(out=w_raw[a], in_=w_rows[a])
+        nc.sync.dma_start(out=w_raw[1], in_=w_rows[1])
         nc.sync.dma_start(out=bias[:], in_=b)
         nc.sync.dma_start(pos_sb[0][:], pos1)
         nc.sync.dma_start(pos_sb[1][:], pos2)
@@ -66,7 +64,7 @@ def tile_picked_sub_lin_silu_sub_e_kernel(tc, xT, w, b, gate, offs, pos1, pos2, 
         nc.scalar.activation(warm_out[:], warm_in[:], SILU)
 
         picked0 = keep.tile([P, 2, PACK, HALF], BF16, name="picked0")
-        picked1 = keep.tile([P, 3, 3, THIRD], BF16, name="picked1")
+        picked1 = keep.tile([P, 4, 2, QUARTER], BF16, name="picked1")
         grouped = [keep.tile([P, S, PACK], BF16, name="grouped%d" % a, align_bytes=64) for a in range(PASSES)]
         x_codes = [keep.tile([P, S], U32, name="x_codes%d" % a, align_bytes=64) for a in range(PASSES)]
         scales0 = keep.tile([P, S], U8, name="x_scales0", align_bytes=64)
@@ -104,7 +102,7 @@ def tile_picked_sub_lin_silu_sub_e_kernel(tc, xT, w, b, gate, offs, pos1, pos2, 
                 in_=w_grouped[:, a].rearrange("p n t -> p (n t)"),
             )
 
-        starts = [2 * GROUP, 3 * GROUP, 0, GROUP, 4 * GROUP, 5 * GROUP]
+        starts = [0, GROUP, 3 * GROUP, 2 * GROUP, 4 * GROUP, 5 * GROUP]
         groups = [slice(s, s + GROUP) for s in starts]
         acc = [psum.tile([P, GROUP], F32, name="acc%d" % g) for g in range(len(groups))]
 
@@ -120,46 +118,61 @@ def tile_picked_sub_lin_silu_sub_e_kernel(tc, xT, w, b, gate, offs, pos1, pos2, 
                 stop=(a == PASSES - 1),
             )
 
+        def pair_views(u, h):
+            return (
+                grouped[0][:, h * HALF : (h + 1) * HALF, 2 * u : 2 * u + 2],
+                picked0[:, h, 2 * u : 2 * u + 2, :].rearrange("p t i -> p i t"),
+            )
+
         for u in range(2):
             for h in range(2):
                 scalar_gather(picked0[:, h, 2 * u, :], twin[u][:], h * HALF, (h + 1) * HALF)
             vector_gather(picked0[:, :, 2 * u + 1, :], twin[u][:, T:], 0, S)
-        for h in range(2):
-            nc.vector.tensor_copy(
-                grouped[0][:, h * HALF : (h + 1) * HALF, :].rearrange("p (c i) t -> p c t i", i=4),
-                picked0[:, h].rearrange("p t (c i) -> p c t i", i=4),
-            )
+            nc.vector.tensor_copy(*pair_views(u, 0))
+            if u == 0:
+                nc.vector.tensor_copy(*pair_views(u, 1))
+                nc.vector.tensor_copy(*w_views(0))
+                quantize_w(0)
+            else:
+                nc.scalar.copy(*pair_views(u, 1))
         for h in range(2):
             quantize(0, scales0, h * HALF, (h + 1) * HALF)
-
-        for c in (1, 2, 0):
-            scalar_gather(picked1[:, c, 0, :], twin[2][:], c * THIRD, (c + 1) * THIRD)
-        vector_gather(picked1[:, :, 1, :], twin[2][:, T:], 0, S)
-        nc.vector.tensor_copy(
-            grouped[1][:, THIRD:S, 0:2].rearrange("p (c i) t -> p c i t", c=2),
-            picked1[:, 1:3, 0:2, :].rearrange("p c t i -> p c i t"),
-        )
-        scalar_gather(picked1[:, 0, 2, :], lone[0][:], 0, THIRD)
-        scalar_gather(last_pair[:, 0, :], lone[0][:], THIRD, S)
-        nc.vector.tensor_copy(grouped[1][:, 0:THIRD, 0:3], picked1[:, 0].rearrange("p t i -> p i t"))
-
-        def staged(lo):
-            vector_gather(last_pair[:, 1, lo - THIRD : lo - THIRD + GROUP], lone[1][:], lo, lo + GROUP)
-            nc.scalar.copy(
-                grouped[1][:, lo : lo + GROUP, 2:4],
-                last_pair[:, :, lo - THIRD : lo - THIRD + GROUP].rearrange("p t n -> p n t"),
-            )
-
-        staged(2 * GROUP)
-        staged(3 * GROUP)
-        vector_gather(grouped[1][:, 0:THIRD, 3], lone[1][:], 0, THIRD)
-        nc.gpsimd.tensor_scalar(*w_views(0), 1.0, 0.0, MULT, ADD)
-        quantize_w(0)
         for g in range(len(groups)):
             multiply(0, scales0, g)
-        nc.scalar.copy(*w_views(1))
-        staged(4 * GROUP)
-        staged(5 * GROUP)
+
+        for c in range(4):
+            scalar_gather(picked1[:, c, 0, :], twin[2][:], c * QUARTER, (c + 1) * QUARTER)
+        for h in range(2):
+            vector_gather(picked1[:, 2 * h : 2 * h + 2, 1, :], twin[2][:, T:], h * HALF, (h + 1) * HALF)
+
+        def early_pair(h):
+            return (
+                grouped[1][:, h * HALF : (h + 1) * HALF, 0:2].rearrange("p (c i) t -> p c i t", c=2),
+                picked1[:, 2 * h : 2 * h + 2].rearrange("p c t i -> p c i t"),
+            )
+
+        nc.vector.tensor_copy(*early_pair(0))
+        nc.gpsimd.tensor_scalar(*early_pair(1), 1.0, 0.0, MULT, ADD)
+        vector_gather(grouped[1][:, 0:IN_PLACE, 2], lone[0][:], 0, IN_PLACE)
+        scalar_gather(last_pair[:, 0, :], lone[0][:], IN_PLACE, S)
+
+        def stage_last(gather, lo):
+            gather(last_pair[:, 1, lo - IN_PLACE : lo - IN_PLACE + GROUP], lone[1][:], lo, lo + GROUP)
+
+        def place(lo):
+            nc.scalar.copy(
+                grouped[1][:, lo : lo + GROUP, 2:4],
+                last_pair[:, :, lo - IN_PLACE : lo - IN_PLACE + GROUP].rearrange("p t n -> p n t"),
+            )
+
+        vector_gather(grouped[1][:, 0:IN_PLACE, 3], lone[1][:], 0, IN_PLACE)
+        stage_last(scalar_gather, 3 * GROUP)
+        stage_last(scalar_gather, 4 * GROUP)
+        place(3 * GROUP)
+        stage_last(scalar_gather, 5 * GROUP)
+        place(4 * GROUP)
+        place(5 * GROUP)
+        nc.gpsimd.tensor_scalar(*w_views(1), 1.0, 0.0, MULT, ADD)
         scales1 = keep.tile([P, S], U8, name="x_scales1", tag="w_raw1", align_bytes=64)
         quantize_w(1)
         for g, cols in enumerate(groups):
@@ -185,13 +198,13 @@ def tile_picked_sub_lin_silu_sub_e_kernel(tc, xT, w, b, gate, offs, pos1, pos2, 
             nc.vector.tensor_tensor(result[:, lo:hi], first[:, lo:hi], second[:, lo:hi], ADD)
             nc.sync.dma_start(out=out[:, lo:hi], in_=result[:, lo:hi])
 
-        for lo, hi in ((0, piece), (piece, V)):
-            nc.scalar.activation(fetched[:, lo:hi], y[:].indirect(pos_sb[1][:, lo // LIST : hi // LIST]), COPY)
-        fetch_first(0, piece)
+        for lo in range(0, V, piece):
+            nc.scalar.activation(fetched[:, lo : lo + piece], y[:].indirect(pos_sb[1][:, lo // LIST : (lo + piece) // LIST]), COPY)
+        fetch_first(0, 2 * piece)
         weigh_second(0, piece)
-        fetch_first(piece, 2 * piece)
-        add_and_store(0, piece)
-        weigh_second(piece, V)
         fetch_first(2 * piece, V)
+        add_and_store(0, piece)
+        weigh_second(piece, 2 * piece)
+        weigh_second(2 * piece, V)
         add_and_store(piece, 2 * piece)
         add_and_store(2 * piece, V)

@@ -47,7 +47,7 @@ def tile_picked_sub_lin_silu_sub_e_kernel(tc, xT, w, b, gate, offs, pos1, pos2, 
         w_rows = w.rearrange("(a p t) n -> a p t n", p=P, t=PACK)
         nc.sync.dma_start(out=twin[0][:], in_=x_pairs[0, 0])
         nc.sync.dma_start(offs_sb[:], offs)
-        nc.sync.dma_start(out=w_raw[0], in_=w_rows[0])
+        nc.scalar.dma_start(out=w_raw[0], in_=w_rows[0])
         nc.sync.dma_start(out=twin[1][:], in_=x_pairs[0, 1])
         nc.sync.dma_start(out=twin[2][:], in_=x_pairs[1, 0])
         for j in range(2):

@@ -145,14 +145,15 @@ def tile_picked_sub_lin_silu_sub_e_kernel(tc, xT, w, b, gate, offs, pos1, pos2, 
         for h in range(2):
             vector_gather(picked1[:, 2 * h : 2 * h + 2, 1, :], twin[2][:, T:], h * HALF, (h + 1) * HALF)
 
-        def early_pair(h):
+        def early_pair(c0, c1):
             return (
-                grouped[1][:, h * HALF : (h + 1) * HALF, 0:2].rearrange("p (c i) t -> p c i t", c=2),
-                picked1[:, 2 * h : 2 * h + 2].rearrange("p c t i -> p c i t"),
+                grouped[1][:, c0 * QUARTER : c1 * QUARTER, 0:2].rearrange("p (c i) t -> p c i t", i=QUARTER),
+                picked1[:, c0:c1].rearrange("p c t i -> p c i t"),
             )
 
-        nc.vector.tensor_copy(*early_pair(0))
-        nc.gpsimd.tensor_scalar(*early_pair(1), 1.0, 0.0, MULT, ADD)
+        nc.vector.tensor_copy(*early_pair(0, 2))
+        nc.scalar.copy(*early_pair(2, 3))
+        nc.gpsimd.tensor_scalar(*early_pair(3, 4), 1.0, 0.0, MULT, ADD)
         vector_gather(grouped[1][:, 0:IN_PLACE, 2], lone[0][:], 0, IN_PLACE)
         scalar_gather(last_pair[:, 0, :], lone[0][:], IN_PLACE, S)
 

@@ -84,8 +84,8 @@ def tile_picked_sub_lin_silu_sub_e_kernel(tc, xT, w, b, gate, offs, pos1, pos2, 
 
         def w_views(a):
             return (
-                w_grouped[:, a].rearrange("p (c i) t -> p c t i", i=4),
-                w_raw[a].rearrange("p t (c i) -> p c t i", i=4),
+                w_grouped[:, a].rearrange("p (c i) t -> p c t i", i=2),
+                w_raw[a].rearrange("p t (c i) -> p c t i", i=2),
             )
 
         def quantize(a, scales, lo, hi):

@@ -23,7 +23,7 @@ GROUP = 128
 LIST = 16
 HALF = S // 2
 QUARTER = S // 4
-IN_PLACE = S // 2
+IN_PLACE = 416
 
 
 def tile_picked_sub_lin_silu_sub_e_kernel(tc, xT, w, b, gate, offs, pos1, pos2, out):
@@ -102,8 +102,7 @@ def tile_picked_sub_lin_silu_sub_e_kernel(tc, xT, w, b, gate, offs, pos1, pos2, 
                 in_=w_grouped[:, a].rearrange("p n t -> p (n t)"),
             )
 
-        starts = [0, GROUP, 3 * GROUP, 2 * GROUP, 4 * GROUP, 5 * GROUP]
-        groups = [slice(s, s + GROUP) for s in starts]
+        groups = [slice(s, s + GROUP) for s in range(0, S, GROUP)]
         acc = [psum.tile([P, GROUP], F32, name="acc%d" % g) for g in range(len(groups))]
 
         def multiply(a, scales, g):
@@ -157,22 +156,26 @@ def tile_picked_sub_lin_silu_sub_e_kernel(tc, xT, w, b, gate, offs, pos1, pos2, 
         vector_gather(grouped[1][:, 0:IN_PLACE, 2], lone[0][:], 0, IN_PLACE)
         scalar_gather(last_pair[:, 0, :], lone[0][:], IN_PLACE, S)
 
-        def stage_last(gather, lo):
-            gather(last_pair[:, 1, lo - IN_PLACE : lo - IN_PLACE + GROUP], lone[1][:], lo, lo + GROUP)
+        borders = (IN_PLACE, 4 * GROUP, 5 * GROUP, S)
 
-        def place(lo):
+        def stage_last(j):
+            lo, hi = borders[j], borders[j + 1]
+            scalar_gather(last_pair[:, 1, lo - IN_PLACE : hi - IN_PLACE], lone[1][:], lo, hi)
+
+        def place(j):
+            lo, hi = borders[j], borders[j + 1]
             nc.scalar.copy(
-                grouped[1][:, lo : lo + GROUP, 2:4],
-                last_pair[:, :, lo - IN_PLACE : lo - IN_PLACE + GROUP].rearrange("p t n -> p n t"),
+                grouped[1][:, lo:hi, 2:4],
+                last_pair[:, :, lo - IN_PLACE : hi - IN_PLACE].rearrange("p t n -> p n t"),
             )
 
         vector_gather(grouped[1][:, 0:IN_PLACE, 3], lone[1][:], 0, IN_PLACE)
-        stage_last(scalar_gather, 3 * GROUP)
-        stage_last(scalar_gather, 4 * GROUP)
-        place(3 * GROUP)
-        stage_last(scalar_gather, 5 * GROUP)
-        place(4 * GROUP)
-        place(5 * GROUP)
+        stage_last(0)
+        stage_last(1)
+        place(0)
+        stage_last(2)
+        place(1)
+        place(2)
         nc.gpsimd.tensor_scalar(*w_views(1), 1.0, 0.0, MULT, ADD)
         scales1 = keep.tile([P, S], U8, name="x_scales1", tag="w_raw1", align_bytes=64)
         quantize_w(1)

from contextlib import ExitStack

import concourse.mybir as mybir

K, T, D, S, V, N = 1024, 2048, 2, 768, 384, 128
FLOPS = 2 * K * N * S

F32 = mybir.dt.float32
BF16 = mybir.dt.bfloat16
U32 = mybir.dt.uint32
U16 = mybir.dt.uint16
U8 = mybir.dt.uint8
FP8X4 = mybir.dt.float8_e4m3fn_x4
SILU = mybir.ActivationFunctionType.Silu
COPY = mybir.ActivationFunctionType.Copy
MULT = mybir.AluOpType.mult
ADD = mybir.AluOpType.add

P = 128
PACK = 4
PASSES = K // (P * PACK)
GROUP = 128
LIST = 16
HALF = S // 2
QUARTER = S // 4
IN_PLACE = 416


def tile_picked_sub_lin_silu_sub_e_kernel(tc, xT, w, b, gate, offs, pos1, pos2, out):
    nc = tc.nc
    with ExitStack() as ctx:
        keep = ctx.enter_context(tc.tile_pool(name="keep", bufs=1))
        psum = ctx.enter_context(tc.psum_pool(name="psum", bufs=1))

        offs_sb = keep.tile([P, S // LIST], U16, name="offs_sb")
        pos_sb = [keep.tile([P, V // LIST], U16, name="pos_sb%d" % d) for d in range(D)]
        twin = [keep.tile([P, 2 * T], F32, name="twin%d" % j, align_bytes=64) for j in range(3)]
        lone = [keep.tile([P, T], F32, name="lone%d" % j, align_bytes=64) for j in range(2)]
        staged_n = S - IN_PLACE
        last_pair = keep.tile([P, 2, staged_n], BF16, name="last_pair")
        w_raw = [keep.tile([P, PACK, N], F32, name="w_raw%d" % a, tag="w_raw%d" % a, align_bytes=64)[:] for a in range(PASSES)]
        bias = keep.tile([P, 1], F32, name="bias")
        gate_sb = keep.tile([P, D, V], F32, name="gate_sb")

        x_pairs = xT.rearrange("(a p u t) n -> a u p (t n)", p=P, u=2, t=2)
        x_rows = xT.rearrange("(a p t) n -> a t p n", p=P, t=PACK)
        w_rows = w.rearrange("(a p t) n -> a p t n", p=P, t=PACK)
        nc.sync.dma_start(out=twin[0][:], in_=x_pairs[0, 0])
        nc.sync.dma_start(offs_sb[:], offs)
        nc.scalar.dma_start(out=w_raw[0], in_=w_rows[0])
        nc.sync.dma_start(out=twin[1][:], in_=x_pairs[0, 1])
        nc.sync.dma_start(out=twin[2][:], in_=x_pairs[1, 0])
        for j in range(2):
            nc.sync.dma_start(out=lone[j][:], in_=x_rows[1, 2 + j])
        nc.sync.dma_start(out=w_raw[1], in_=w_rows[1])
        nc.sync.dma_start(out=bias[:], in_=b)
        nc.sync.dma_start(pos_sb[0][:], pos1)
        nc.sync.dma_start(pos_sb[1][:], pos2)
        nc.sync.dma_start(out=gate_sb[:], in_=gate.rearrange("d p v -> p d v"))

        warm_in = keep.tile([P, 1], F32, name="warm_in")
        warm_out = keep.tile([P, 1], F32, name="warm_out")
        nc.vector.memset(warm_in[:], 0.0)
        nc.scalar.activation(warm_out[:], warm_in[:], SILU)

        picked0 = keep.tile([P, 2, PACK, HALF], BF16, name="picked0")
        picked1 = keep.tile([P, 4, 2, QUARTER], BF16, name="picked1")
        grouped = [keep.tile([P, S, PACK], BF16, name="grouped%d" % a, align_bytes=64) for a in range(PASSES)]
        x_codes = [keep.tile([P, S], U32, name="x_codes%d" % a, align_bytes=64) for a in range(PASSES)]
        scales0 = keep.tile([P, S], U8, name="x_scales0", align_bytes=64)
        w_grouped = keep.tile([P, PASSES, N, PACK], BF16, name="w_grouped", align_bytes=64)
        w_codes = keep.tile([P, PASSES * N], U32, name="w_codes", align_bytes=64)
        w_scales = keep.tile([P, PASSES * N], U8, name="w_scales", align_bytes=64)
        y = keep.tile([P, S], F32, name="y")

        def entries(lo, hi):
            return offs_sb[:, lo // LIST : hi // LIST]

        def scalar_gather(dst, window, lo, hi):
            nc.scalar.activation(dst, window.indirect(entries(lo, hi)), COPY)

        def vector_gather(dst, window, lo, hi):
            nc.vector.tensor_copy(dst, window.indirect(entries(lo, hi)))

        def w_views(a):
            return (
                w_grouped[:, a].rearrange("p (c i) t -> p c t i", i=2),
                w_raw[a].rearrange("p t (c i) -> p c t i", i=2),
            )

        def quantize(a, scales, lo, hi):
            nc.vector.quantize_mx(
                out=x_codes[a][:, lo:hi].bitcast(FP8X4),
                scales=scales[:, lo:hi],
                in_=grouped[a][:, lo:hi, :].rearrange("p n t -> p (n t)"),
            )

        def quantize_w(a):
            nc.vector.quantize_mx(
                out=w_codes[:, a * N : (a + 1) * N].bitcast(FP8X4),
                scales=w_scales[:, a * N : (a + 1) * N],
                in_=w_grouped[:, a].rearrange("p n t -> p (n t)"),
            )

        groups = [slice(s, s + GROUP) for s in range(0, S, GROUP)]
        acc = [psum.tile([P, GROUP], F32, name="acc%d" % g) for g in range(len(groups))]

        def multiply(a, scales, g):
            cols = groups[g]
            nc.tensor.matmul_mx(
                out=acc[g][:],
                lhsT=w_codes[:, a * N : (a + 1) * N].bitcast(FP8X4),
                lhsT_scale=w_scales[:, a * N : (a + 1) * N],
                rhs=x_codes[a][:, cols].bitcast(FP8X4),
                rhs_scale=scales[:, cols],
                start=(a == 0),
                stop=(a == PASSES - 1),
            )

        def pair_views(u, h):
            return (
                grouped[0][:, h * HALF : (h + 1) * HALF, 2 * u : 2 * u + 2],
                picked0[:, h, 2 * u : 2 * u + 2, :].rearrange("p t i -> p i t"),
            )

        for u in range(2):
            for h in range(2):
                scalar_gather(picked0[:, h, 2 * u, :], twin[u][:], h * HALF, (h + 1) * HALF)
            vector_gather(picked0[:, :, 2 * u + 1, :], twin[u][:, T:], 0, S)
            nc.vector.tensor_copy(*pair_views(u, 0))
            if u == 0:
                nc.vector.tensor_copy(*pair_views(u, 1))
                nc.vector.tensor_copy(*w_views(0))
                quantize_w(0)
            else:
                nc.scalar.copy(*pair_views(u, 1))
        for h in range(2):
            quantize(0, scales0, h * HALF, (h + 1) * HALF)
        for g in range(len(groups)):
            multiply(0, scales0, g)

        for c in range(4):
            scalar_gather(picked1[:, c, 0, :], twin[2][:], c * QUARTER, (c + 1) * QUARTER)
        for h in range(2):
            vector_gather(picked1[:, 2 * h : 2 * h + 2, 1, :], twin[2][:, T:], h * HALF, (h + 1) * HALF)

        def early_pair(c0, c1):
            return (
                grouped[1][:, c0 * QUARTER : c1 * QUARTER, 0:2].rearrange("p (c i) t -> p c i t", i=QUARTER),
                picked1[:, c0:c1].rearrange("p c t i -> p c i t"),
            )

        nc.vector.tensor_copy(*early_pair(0, 2))
        nc.scalar.copy(*early_pair(2, 3))
        nc.gpsimd.tensor_scalar(*early_pair(3, 4), 1.0, 0.0, MULT, ADD)
        vector_gather(grouped[1][:, 0:IN_PLACE, 2], lone[0][:], 0, IN_PLACE)
        scalar_gather(last_pair[:, 0, :], lone[0][:], IN_PLACE, S)

        borders = (IN_PLACE, 4 * GROUP, 5 * GROUP, S)

        def stage_last(j):
            lo, hi = borders[j], borders[j + 1]
            scalar_gather(last_pair[:, 1, lo - IN_PLACE : hi - IN_PLACE], lone[1][:], lo, hi)

        def place(j):
            lo, hi = borders[j], borders[j + 1]
            nc.scalar.copy(
                grouped[1][:, lo:hi, 2:4],
                last_pair[:, :, lo - IN_PLACE : hi - IN_PLACE].rearrange("p t n -> p n t"),
            )

        vector_gather(grouped[1][:, 0:IN_PLACE, 3], lone[1][:], 0, IN_PLACE)
        stage_last(0)
        stage_last(1)
        place(0)
        stage_last(2)
        place(1)
        place(2)
        nc.gpsimd.tensor_scalar(*w_views(1), 1.0, 0.0, MULT, ADD)
        scales1 = keep.tile([P, S], U8, name="x_scales1", tag="w_raw1", align_bytes=64)
        quantize_w(1)
        for g, cols in enumerate(groups):
            quantize(1, scales1, cols.start, cols.stop)
            multiply(1, scales1, g)
            nc.scalar.activation(y[:, cols], acc[g][:], SILU, bias=bias[:])

        first = keep.tile([P, V], F32, name="first")
        fetched = keep.tile([P, V], F32, name="fetched")
        second = keep.tile([P, V], F32, name="second")
        result = keep.tile([P, V], F32, name="result")
        piece = V // 3

        def fetch_first(lo, hi):
            nc.vector.tensor_tensor(
                first[:, lo:hi], y[:].indirect(pos_sb[0][:, lo // LIST : hi // LIST]), gate_sb[:, 0, lo:hi], MULT
            )

        def weigh_second(lo, hi):
            nc.vector.tensor_tensor(second[:, lo:hi], fetched[:, lo:hi], gate_sb[:, 1, lo:hi], MULT)

        def add_and_store(lo, hi):
            nc.vector.tensor_tensor(result[:, lo:hi], first[:, lo:hi], second[:, lo:hi], ADD)
            nc.sync.dma_start(out=out[:, lo:hi], in_=result[:, lo:hi])

        for lo in range(0, V, piece):
            nc.scalar.activation(fetched[:, lo : lo + piece], y[:].indirect(pos_sb[1][:, lo // LIST : (lo + piece) // LIST]), COPY)
        fetch_first(0, 2 * piece)
        weigh_second(0, piece)
        fetch_first(2 * piece, V)
        add_and_store(0, piece)
        weigh_second(piece, 2 * piece)
        weigh_second(2 * piece, V)
        add_and_store(piece, 2 * piece)
        add_and_store(2 * piece, V)
